import numpy as np
CORES = [1,9,17,25,33,41,49,57,65,73,81,89,97,105,113,121]
N = 16
def setup_inputs(rng):
    return {"x": rng.standard_normal((N, 128, 2048), dtype=np.float32)}
def reference(x):
    s = x.sum(axis=0, dtype=np.float64).astype(x.dtype)
    b = 2048 // N
    return {"y": np.stack([s[:, r * b:(r + 1) * b] for r in range(N)])}

@@ -1,0 +1,177 @@
+import concourse.bass as bass
+import concourse.mybir as mybir
+
+MODE = "sbuf"
+Q = 1
+E = 1
+FWD = [4, 5, 6, 7]
+FA = [0]
+FB = [3]
+
+W = 128 // Q
+NCALL = Q * E
+JPER = 8 // NCALL
+
+SCRATCH = {
+    "xs": ("sbuf", [128, 2048], "float32") if MODE == "sbuf" else ("dram", [16 * Q, 128, W], "float32"),
+    "fw": ("dram", [8 * Q, 128, W], "float32"),
+    "la": ("dram", [16 * Q, 128, W], "float32"),
+    "res": ("dram", [2 * Q, 128, W], "float32"),
+}
+SEMAPHORES = ["st", "snt", "ra", "rb", "fa", "fb"] + ["f%d" % c for c in range(8)] + ["l%d" % c for c in range(8)]
+
+
+def sem_f(T, c):
+    return [T.sem.f0, T.sem.f1, T.sem.f2, T.sem.f3, T.sem.f4, T.sem.f5, T.sem.f6, T.sem.f7][c]
+
+
+def sem_l(T, c):
+    return [T.sem.l0, T.sem.l1, T.sem.l2, T.sem.l3, T.sem.l4, T.sem.l5, T.sem.l6, T.sem.l7][c]
+
+
+def groups(k):
+    rot = [(k + 1 + i) % 8 for i in range(8)]
+    return [rot[c * JPER:(c + 1) * JPER] for c in range(NCALL)]
+
+
+def fwd_plan(k):
+    out, n = [], 0
+    for js in groups(k):
+        per = {}
+        for j in js:
+            for q in range(Q):
+                if j != k:
+                    per.setdefault(FWD[n % len(FWD)], []).append((j, q))
+                    n += 1
+        out.append(per)
+    return out
+
+
+def fwd_engines(n):
+    e = 8
+    while e * n > 8:
+        e //= 2
+    return e
+
+
+def xfer(topo, dst_core, mask, sem, src, dst):
+    rid, pid, se = topo.addr(dst_core)
+    return bass.RemoteDMATransfer(dst_ids=[bass.DstId(rid=rid, pnc=pid)], dma_engine_mask=mask, remote_sem=sem,
+                                  src=src, dst=dst)
+
+
+def fold(topo, dst_core, mask, sem, srcs, dst):
+    rid, pid, se = topo.addr(dst_core)
+    return bass.RemoteDMATransfer(dst_ids=[bass.DstId(rid=rid, pnc=pid)], dma_engine_mask=mask, remote_sem=sem,
+                                  srcs=srcs, dsts=[dst], alu_op=1)
+
+
+def rank_core(g, T, topo, k, p):
+    base = (2 * k + p) * 8
+    gs = groups(k)
+    plan = fwd_plan(k)
+    where = {}
+    for c in range(NCALL):
+        for f, lst in plan[c].items():
+            for jq in lst:
+                where[jq] = f
+
+    def load(c):
+        n = 0
+        if MODE == "sbuf":
+            runs = []
+            for j in sorted(gs[c]):
+                if runs and runs[-1][1] == j:
+                    runs[-1][1] = j + 1
+                else:
+                    runs.append([j, j + 1])
+            for a, b in runs:
+                g.dma_start(T.xs[:, 256 * a:256 * b], T.x[:, 256 * a:256 * b]).then_inc(sem_l(T, c), 16)
+                n += 16
+        else:
+            for j in gs[c]:
+                for b in (2 * j + 1 - p, 2 * j + p):
+                    out = T.xs[b] if Q == 1 else T.xs[b * Q:(b + 1) * Q]
+                    g.dma_start(out, T.x[:, 128 * b:128 * (b + 1)]).then_inc(sem_l(T, c), 16)
+                    n += 16
+        return n
+
+    def piece(b, q):
+        return T.xs[:, 128 * b:128 * (b + 1)] if MODE == "sbuf" else T.xs[b * Q + q]
+
+    loaded = [load(0)]
+    sent = 0
+    for c in range(NCALL):
+        if c + 1 < NCALL:
+            loaded.append(load(c + 1))
+        g.wait_ge(sem_l(T, c), loaded[c])
+        tr = []
+        ea, eb = 0, 8
+        for j in gs[c]:
+            for q in range(Q):
+                tr.append(xfer(topo, (2 * j + p) * 8 + FA[q], ((1 << E) - 1) << ea, T.sem.fa,
+                               piece(2 * j + p, q), T.la[q * 8 + k]))
+                ea += E
+                m = ((1 << E) - 1) << eb
+                eb += E
+                if j == k:
+                    tr.append(xfer(topo, base + FB[q], m, T.sem.fb, piece(2 * j + 1 - p, q), T.la[(Q + q) * 8 + k]))
+                else:
+                    tr.append(xfer(topo, base + where[(j, q)], m, sem_f(T, c), piece(2 * j + 1 - p, q),
+                                   T.fw[j * Q + q]))
+        g.remote_dma_fused(tr, local_sem=T.sem.snt)
+        sent += 16
+    g.wait_ge(T.sem.ra, 16 * Q)
+    g.dma_start(T.y[:], T.res[0] if Q == 1 else T.res[0:Q]).then_inc(T.sem.st, 16)
+    g.wait_ge(T.sem.rb, 8 * Q)
+    g.wait_ge(T.sem.st, 16)
+    g.dma_start(T.y[:], T.res[1] if Q == 1 else T.res[Q:2 * Q], accum_op=mybir.AluOpType.add,
+                max_dma_last_dim=8192).then_inc(T.sem.st, 16)
+    g.wait_ge(T.sem.snt, sent)
+    g.wait_ge(T.sem.st, 32)
+
+
+def helper_core(g, T, topo, k, p, me):
+    base = (2 * k + p) * 8
+    sent = 0
+    if me in FWD:
+        plan = fwd_plan(k)
+        for c in range(NCALL):
+            lst = plan[c].get(me, [])
+            if not lst:
+                continue
+            g.wait_ge(sem_f(T, c), E * len(lst))
+            e = fwd_engines(len(lst))
+            tr = [xfer(topo, (2 * j + p) * 8 + FB[q], ((1 << e) - 1) << (i * e), T.sem.fb, T.fw[j * Q + q],
+                       T.la[(Q + q) * 8 + k]) for i, (j, q) in enumerate(lst)]
+            g.remote_dma_fused(tr, local_sem=T.sem.snt)
+            sent += e * len(lst)
+    for q in range(Q):
+        if FA[q] == me:
+            g.wait_ge(T.sem.fa, 8 * E)
+            g.remote_dma_fused([fold(topo, base + 1, 0xFFFF, T.sem.ra, [T.la[q * 8 + s] for s in range(8)], T.res[q])],
+                               local_sem=T.sem.snt)
+            sent += 16
+    for q in range(Q):
+        if FB[q] == me:
+            n = E
+            for s in range(8):
+                if s != k:
+                    for per in fwd_plan(s):
+                        for lst in per.values():
+                            if (k, q) in lst:
+                                n += fwd_engines(len(lst))
+            g.wait_ge(T.sem.fb, n)
+            g.remote_dma_fused([fold(topo, (base ^ 8) + 1, 0x00FF, T.sem.rb, [T.la[(Q + q) * 8 + s] for s in range(8)],
+                                     T.res[Q + q])], local_sem=T.sem.snt)
+            sent += 8
+    if sent:
+        g.wait_ge(T.sem.snt, sent)
+
+
+def rank_program(g, core, T, topo):
+    ch, me = core // 8, core % 8
+    if me == 1:
+        rank_core(g, T, topo, ch // 2, ch % 2)
+    else:
+        helper_core(g, T, topo, ch // 2, ch % 2, me)

@@ -1,24 +1,19 @@
 import concourse.bass as bass
 import concourse.mybir as mybir
 
-MODE = "sbuf"
-Q = 1
 E = 1
 FWD = [4, 5, 6, 7]
-FA = [0]
-FB = [3]
-
-W = 128 // Q
-NCALL = Q * E
-JPER = 8 // NCALL
+FA = 0
+FB = 3
+JPER = 8 // E
 
 SCRATCH = {
-    "xs": ("sbuf", [128, 2048], "float32") if MODE == "sbuf" else ("dram", [16 * Q, 128, W], "float32"),
-    "fw": ("dram", [8 * Q, 128, W], "float32"),
-    "la": ("dram", [16 * Q, 128, W], "float32"),
-    "res": ("dram", [2 * Q, 128, W], "float32"),
+    "xs": ("sbuf", [128, 2048], "float32"),
+    "fw": ("dram", [8, 128, 128], "float32"),
+    "la": ("dram", [8, 128, 128], "float32"),
+    "res": ("dram", [2, 128, 128], "float32"),
 }
-SEMAPHORES = ["st", "snt", "ra", "rb", "fa", "fb"] + ["f%d" % c for c in range(8)] + ["l%d" % c for c in range(8)]
+SEMAPHORES = ["st", "snt", "ra", "rb", "arr"] + ["f%d" % c for c in range(8)] + ["l%d" % c for c in range(8)]
 
 
 def sem_f(T, c):
@@ -31,7 +26,7 @@ def sem_l(T, c):
 
 def groups(k):
     rot = [(k + 1 + i) % 8 for i in range(8)]
-    return [rot[c * JPER:(c + 1) * JPER] for c in range(NCALL)]
+    return [rot[c * JPER:(c + 1) * JPER] for c in range(E)]
 
 
 def fwd_plan(k):
@@ -39,10 +34,9 @@ def fwd_plan(k):
     for js in groups(k):
         per = {}
         for j in js:
-            for q in range(Q):
-                if j != k:
-                    per.setdefault(FWD[n % len(FWD)], []).append((j, q))
-                    n += 1
+            if j != k:
+                per.setdefault(FWD[n % len(FWD)], []).append(j)
+                n += 1
         out.append(per)
     return out
 
@@ -71,63 +65,45 @@ def rank_core(g, T, topo, k, p):
     gs = groups(k)
     plan = fwd_plan(k)
     where = {}
-    for c in range(NCALL):
+    for c in range(E):
         for f, lst in plan[c].items():
-            for jq in lst:
-                where[jq] = f
+            for j in lst:
+                where[j] = f
 
     def load(c):
-        n = 0
-        if MODE == "sbuf":
-            runs = []
-            for j in sorted(gs[c]):
-                if runs and runs[-1][1] == j:
-                    runs[-1][1] = j + 1
-                else:
-                    runs.append([j, j + 1])
-            for a, b in runs:
-                g.dma_start(T.xs[:, 256 * a:256 * b], T.x[:, 256 * a:256 * b]).then_inc(sem_l(T, c), 16)
-                n += 16
-        else:
-            for j in gs[c]:
-                for b in (2 * j + 1 - p, 2 * j + p):
-                    out = T.xs[b] if Q == 1 else T.xs[b * Q:(b + 1) * Q]
-                    g.dma_start(out, T.x[:, 128 * b:128 * (b + 1)]).then_inc(sem_l(T, c), 16)
-                    n += 16
-        return n
+        runs = []
+        for j in sorted(gs[c]):
+            if runs and runs[-1][1] == j:
+                runs[-1][1] = j + 1
+            else:
+                runs.append([j, j + 1])
+        for a, b in runs:
+            g.dma_start(T.xs[:, 256 * a:256 * b], T.x[:, 256 * a:256 * b]).then_inc(sem_l(T, c), 16)
+        return 16 * len(runs)
 
-    def piece(b, q):
-        return T.xs[:, 128 * b:128 * (b + 1)] if MODE == "sbuf" else T.xs[b * Q + q]
+    def block(b):
+        return T.xs[:, 128 * b:128 * (b + 1)]
 
     loaded = [load(0)]
-    sent = 0
-    for c in range(NCALL):
-        if c + 1 < NCALL:
+    for c in range(E):
+        if c + 1 < E:
             loaded.append(load(c + 1))
         g.wait_ge(sem_l(T, c), loaded[c])
         tr = []
-        ea, eb = 0, 8
-        for j in gs[c]:
-            for q in range(Q):
-                tr.append(xfer(topo, (2 * j + p) * 8 + FA[q], ((1 << E) - 1) << ea, T.sem.fa,
-                               piece(2 * j + p, q), T.la[q * 8 + k]))
-                ea += E
-                m = ((1 << E) - 1) << eb
-                eb += E
-                if j == k:
-                    tr.append(xfer(topo, base + FB[q], m, T.sem.fb, piece(2 * j + 1 - p, q), T.la[(Q + q) * 8 + k]))
-                else:
-                    tr.append(xfer(topo, base + where[(j, q)], m, sem_f(T, c), piece(2 * j + 1 - p, q),
-                                   T.fw[j * Q + q]))
+        for i, j in enumerate(gs[c]):
+            m = ((1 << E) - 1) << (i * E)
+            tr.append(xfer(topo, (2 * j + p) * 8 + FB, m, T.sem.arr, block(2 * j + 1 - p), T.la[k]))
+            if j == k:
+                tr.append(xfer(topo, base + FA, m << 8, T.sem.arr, block(2 * j + p), T.la[k]))
+            else:
+                tr.append(xfer(topo, base + where[j], m << 8, sem_f(T, c), block(2 * j + p), T.fw[j]))
         g.remote_dma_fused(tr, local_sem=T.sem.snt)
-        sent += 16
-    g.wait_ge(T.sem.ra, 16 * Q)
-    g.dma_start(T.y[:], T.res[0] if Q == 1 else T.res[0:Q]).then_inc(T.sem.st, 16)
-    g.wait_ge(T.sem.rb, 8 * Q)
+    g.wait_ge(T.sem.rb, 8)
+    g.dma_start(T.y[:], T.res[0]).then_inc(T.sem.st, 16)
+    g.wait_ge(T.sem.ra, 16)
     g.wait_ge(T.sem.st, 16)
-    g.dma_start(T.y[:], T.res[1] if Q == 1 else T.res[Q:2 * Q], accum_op=mybir.AluOpType.add,
-                max_dma_last_dim=8192).then_inc(T.sem.st, 16)
-    g.wait_ge(T.sem.snt, sent)
+    g.dma_start(T.y[:], T.res[1], accum_op=mybir.AluOpType.add, max_dma_last_dim=8192).then_inc(T.sem.st, 16)
+    g.wait_ge(T.sem.snt, 16 * E)
     g.wait_ge(T.sem.st, 32)
 
 
@@ -136,35 +112,33 @@ def helper_core(g, T, topo, k, p, me):
     sent = 0
     if me in FWD:
         plan = fwd_plan(k)
-        for c in range(NCALL):
+        for c in range(E):
             lst = plan[c].get(me, [])
             if not lst:
                 continue
             g.wait_ge(sem_f(T, c), E * len(lst))
             e = fwd_engines(len(lst))
-            tr = [xfer(topo, (2 * j + p) * 8 + FB[q], ((1 << e) - 1) << (i * e), T.sem.fb, T.fw[j * Q + q],
-                       T.la[(Q + q) * 8 + k]) for i, (j, q) in enumerate(lst)]
+            tr = [xfer(topo, (2 * j + p) * 8 + FA, ((1 << e) - 1) << (i * e), T.sem.arr, T.fw[j], T.la[k])
+                  for i, j in enumerate(lst)]
             g.remote_dma_fused(tr, local_sem=T.sem.snt)
             sent += e * len(lst)
-    for q in range(Q):
-        if FA[q] == me:
-            g.wait_ge(T.sem.fa, 8 * E)
-            g.remote_dma_fused([fold(topo, base + 1, 0xFFFF, T.sem.ra, [T.la[q * 8 + s] for s in range(8)], T.res[q])],
-                               local_sem=T.sem.snt)
-            sent += 16
-    for q in range(Q):
-        if FB[q] == me:
-            n = E
-            for s in range(8):
-                if s != k:
-                    for per in fwd_plan(s):
-                        for lst in per.values():
-                            if (k, q) in lst:
-                                n += fwd_engines(len(lst))
-            g.wait_ge(T.sem.fb, n)
-            g.remote_dma_fused([fold(topo, (base ^ 8) + 1, 0x00FF, T.sem.rb, [T.la[(Q + q) * 8 + s] for s in range(8)],
-                                     T.res[Q + q])], local_sem=T.sem.snt)
-            sent += 8
+    if me == FB:
+        g.wait_ge(T.sem.arr, 8 * E)
+        g.remote_dma_fused([fold(topo, (base ^ 8) + 1, 0x00FF, T.sem.rb, [T.la[s] for s in range(8)], T.res[0])],
+                           local_sem=T.sem.snt)
+        sent += 8
+    if me == FA:
+        n = E
+        for s in range(8):
+            if s != k:
+                for per in fwd_plan(s):
+                    for lst in per.values():
+                        if k in lst:
+                            n += fwd_engines(len(lst))
+        g.wait_ge(T.sem.arr, n)
+        g.remote_dma_fused([fold(topo, base + 1, 0xFFFF, T.sem.ra, [T.la[s] for s in range(8)], T.res[1])],
+                           local_sem=T.sem.snt)
+        sent += 16
     if sent:
         g.wait_ge(T.sem.snt, sent)
 

@@ -1,7 +1,9 @@
 import concourse.bass as bass
 import concourse.mybir as mybir
 
-E = 1
+E = 2
+PB = None
+PA = None
 FWD = [4, 5, 6, 7]
 FA = 0
 FB = 3
@@ -10,7 +12,7 @@ JPER = 8 // E
 SCRATCH = {
     "xs": ("sbuf", [128, 2048], "float32"),
     "fw": ("dram", [8, 128, 128], "float32"),
-    "la": ("dram", [8, 128, 128], "float32"),
+    "la": ("dram", [9, 128, 128], "float32"),
     "res": ("dram", [2, 128, 128], "float32"),
 }
 SEMAPHORES = ["st", "snt", "ra", "rb", "arr"] + ["f%d" % c for c in range(8)] + ["l%d" % c for c in range(8)]
@@ -27,6 +29,10 @@ def sem_l(T, c):
 def groups(k):
     rot = [(k + 1 + i) % 8 for i in range(8)]
     return [rot[c * JPER:(c + 1) * JPER] for c in range(E)]
+
+
+def early(s, j):
+    return j not in groups(s)[-1]
 
 
 def fwd_plan(k):
@@ -46,6 +52,14 @@ def fwd_engines(n):
     while e * n > 8:
         e //= 2
     return e
+
+
+def fwd_count(s, j):
+    for per in fwd_plan(s):
+        for lst in per.values():
+            if j in lst:
+                return fwd_engines(len(lst))
+    return 0
 
 
 def xfer(topo, dst_core, mask, sem, src, dst):
@@ -92,7 +106,8 @@ def rank_core(g, T, topo, k, p):
         tr = []
         for i, j in enumerate(gs[c]):
             m = ((1 << E) - 1) << (i * E)
-            tr.append(xfer(topo, (2 * j + p) * 8 + FB, m, T.sem.arr, block(2 * j + 1 - p), T.la[k]))
+            fb = PB if PB is not None and early(k, j) else FB
+            tr.append(xfer(topo, (2 * j + p) * 8 + fb, m, T.sem.arr, block(2 * j + 1 - p), T.la[k]))
             if j == k:
                 tr.append(xfer(topo, base + FA, m << 8, T.sem.arr, block(2 * j + p), T.la[k]))
             else:
@@ -118,27 +133,25 @@ def helper_core(g, T, topo, k, p, me):
                 continue
             g.wait_ge(sem_f(T, c), E * len(lst))
             e = fwd_engines(len(lst))
-            tr = [xfer(topo, (2 * j + p) * 8 + FA, ((1 << e) - 1) << (i * e), T.sem.arr, T.fw[j], T.la[k])
-                  for i, j in enumerate(lst)]
+            tr = [xfer(topo, (2 * j + p) * 8 + (PA if PA is not None and early(k, j) else FA),
+                       ((1 << e) - 1) << (i * e), T.sem.arr, T.fw[j], T.la[k]) for i, j in enumerate(lst)]
             g.remote_dma_fused(tr, local_sem=T.sem.snt)
             sent += e * len(lst)
-    if me == FB:
-        g.wait_ge(T.sem.arr, 8 * E)
-        g.remote_dma_fused([fold(topo, (base ^ 8) + 1, 0x00FF, T.sem.rb, [T.la[s] for s in range(8)], T.res[0])],
-                           local_sem=T.sem.snt)
-        sent += 8
-    if me == FA:
-        n = E
-        for s in range(8):
-            if s != k:
-                for per in fwd_plan(s):
-                    for lst in per.values():
-                        if k in lst:
-                            n += fwd_engines(len(lst))
-        g.wait_ge(T.sem.arr, n)
-        g.remote_dma_fused([fold(topo, base + 1, 0xFFFF, T.sem.ra, [T.la[s] for s in range(8)], T.res[1])],
-                           local_sem=T.sem.snt)
-        sent += 16
+    for pre, last, cnt, dst, mask, sem, slot in (
+            (PB, FB, lambda s: E, (base ^ 8) + 1, 0x00FF, T.sem.rb, 0),
+            (PA, FA, lambda s: E if s == k else fwd_count(s, k), base + 1, 0xFFFF, T.sem.ra, 1)):
+        first = [s for s in range(8) if pre is not None and early(s, k)]
+        rest = [s for s in range(8) if s not in first]
+        if me == pre:
+            g.wait_ge(T.sem.arr, sum(cnt(s) for s in first))
+            g.remote_dma_fused([fold(topo, base + last, 0xFFFF, T.sem.arr, [T.la[s] for s in first], T.la[8])],
+                               local_sem=T.sem.snt)
+            sent += 16
+        if me == last:
+            g.wait_ge(T.sem.arr, sum(cnt(s) for s in rest) + (16 if first else 0))
+            g.remote_dma_fused([fold(topo, dst, mask, sem, [T.la[s] for s in rest] + ([T.la[8]] if first else []),
+                                     T.res[slot])], local_sem=T.sem.snt)
+            sent += 8 if mask == 0x00FF else 16
     if sent:
         g.wait_ge(T.sem.snt, sent)
 

@@ -2,8 +2,8 @@ import concourse.bass as bass
 import concourse.mybir as mybir
 
 E = 2
-PB = None
-PA = None
+PB = 2
+PA = 7
 FWD = [4, 5, 6, 7]
 FA = 0
 FB = 3

@@ -13,9 +13,9 @@ SCRATCH = {
     "xs": ("sbuf", [128, 2048], "float32"),
     "fw": ("dram", [8, 128, 128], "float32"),
     "la": ("dram", [9, 128, 128], "float32"),
-    "res": ("dram", [2, 128, 128], "float32"),
+    "res": ("dram", [3, 128, 128], "float32"),
 }
-SEMAPHORES = ["st", "snt", "ra", "rb", "arr"] + ["f%d" % c for c in range(8)] + ["l%d" % c for c in range(8)]
+SEMAPHORES = ["st", "snt", "ra", "rb", "rp", "arr"] + ["f%d" % c for c in range(8)] + ["l%d" % c for c in range(8)]
 
 
 def sem_f(T, c):
@@ -106,20 +106,24 @@ def rank_core(g, T, topo, k, p):
         tr = []
         for i, j in enumerate(gs[c]):
             m = ((1 << E) - 1) << (i * E)
-            fb = PB if PB is not None and early(k, j) else FB
-            tr.append(xfer(topo, (2 * j + p) * 8 + fb, m, T.sem.arr, block(2 * j + 1 - p), T.la[k]))
+            tr.append(xfer(topo, (2 * j + p) * 8 + (PB if early(k, j) else FB), m, T.sem.arr, block(2 * j + 1 - p),
+                           T.la[k]))
             if j == k:
                 tr.append(xfer(topo, base + FA, m << 8, T.sem.arr, block(2 * j + p), T.la[k]))
             else:
                 tr.append(xfer(topo, base + where[j], m << 8, sem_f(T, c), block(2 * j + p), T.fw[j]))
         g.remote_dma_fused(tr, local_sem=T.sem.snt)
-    g.wait_ge(T.sem.rb, 8)
+    add = mybir.AluOpType.add
+    g.wait_ge(T.sem.rp, 8)
     g.dma_start(T.y[:], T.res[0]).then_inc(T.sem.st, 16)
-    g.wait_ge(T.sem.ra, 16)
+    g.wait_ge(T.sem.rb, 8)
     g.wait_ge(T.sem.st, 16)
-    g.dma_start(T.y[:], T.res[1], accum_op=mybir.AluOpType.add, max_dma_last_dim=8192).then_inc(T.sem.st, 16)
-    g.wait_ge(T.sem.snt, 16 * E)
+    g.dma_start(T.y[:], T.res[1], accum_op=add, max_dma_last_dim=8192).then_inc(T.sem.st, 16)
+    g.wait_ge(T.sem.ra, 16)
     g.wait_ge(T.sem.st, 32)
+    g.dma_start(T.y[:], T.res[2], accum_op=add, max_dma_last_dim=8192).then_inc(T.sem.st, 16)
+    g.wait_ge(T.sem.snt, 16 * E)
+    g.wait_ge(T.sem.st, 48)
 
 
 def helper_core(g, T, topo, k, p, me):
@@ -133,25 +137,28 @@ def helper_core(g, T, topo, k, p, me):
                 continue
             g.wait_ge(sem_f(T, c), E * len(lst))
             e = fwd_engines(len(lst))
-            tr = [xfer(topo, (2 * j + p) * 8 + (PA if PA is not None and early(k, j) else FA),
-                       ((1 << e) - 1) << (i * e), T.sem.arr, T.fw[j], T.la[k]) for i, j in enumerate(lst)]
+            tr = [xfer(topo, (2 * j + p) * 8 + (PA if early(k, j) else FA), ((1 << e) - 1) << (i * e), T.sem.arr,
+                       T.fw[j], T.la[k]) for i, j in enumerate(lst)]
             g.remote_dma_fused(tr, local_sem=T.sem.snt)
             sent += e * len(lst)
-    for pre, last, cnt, dst, mask, sem, slot in (
-            (PB, FB, lambda s: E, (base ^ 8) + 1, 0x00FF, T.sem.rb, 0),
-            (PA, FA, lambda s: E if s == k else fwd_count(s, k), base + 1, 0xFFFF, T.sem.ra, 1)):
-        first = [s for s in range(8) if pre is not None and early(s, k)]
-        rest = [s for s in range(8) if s not in first]
-        if me == pre:
-            g.wait_ge(T.sem.arr, sum(cnt(s) for s in first))
-            g.remote_dma_fused([fold(topo, base + last, 0xFFFF, T.sem.arr, [T.la[s] for s in first], T.la[8])],
-                               local_sem=T.sem.snt)
-            sent += 16
-        if me == last:
-            g.wait_ge(T.sem.arr, sum(cnt(s) for s in rest) + (16 if first else 0))
-            g.remote_dma_fused([fold(topo, dst, mask, sem, [T.la[s] for s in rest] + ([T.la[8]] if first else []),
-                                     T.res[slot])], local_sem=T.sem.snt)
-            sent += 8 if mask == 0x00FF else 16
+    first = [s for s in range(8) if early(s, k)]
+    rest = [s for s in range(8) if s not in first]
+    if me == PB or me == FB:
+        srcs = first if me == PB else rest
+        g.wait_ge(T.sem.arr, E * len(srcs))
+        g.remote_dma_fused([fold(topo, (base ^ 8) + 1, 0x00FF, T.sem.rp if me == PB else T.sem.rb,
+                                 [T.la[s] for s in srcs], T.res[0 if me == PB else 1])], local_sem=T.sem.snt)
+        sent += 8
+    if me == PA:
+        g.wait_ge(T.sem.arr, sum(fwd_count(s, k) for s in first))
+        g.remote_dma_fused([fold(topo, base + FA, 0xFFFF, T.sem.arr, [T.la[s] for s in first], T.la[8])],
+                           local_sem=T.sem.snt)
+        sent += 16
+    if me == FA:
+        g.wait_ge(T.sem.arr, sum(E if s == k else fwd_count(s, k) for s in rest) + 16)
+        g.remote_dma_fused([fold(topo, base + 1, 0xFFFF, T.sem.ra, [T.la[s] for s in rest] + [T.la[8]], T.res[2])],
+                           local_sem=T.sem.snt)
+        sent += 16
     if sent:
         g.wait_ge(T.sem.snt, sent)
 

import concourse.bass as bass
import concourse.mybir as mybir

E = 2
PB = 2
PA = 7
FWD = [4, 5, 6, 7]
FA = 0
FB = 3
JPER = 8 // E

SCRATCH = {
    "xs": ("sbuf", [128, 2048], "float32"),
    "fw": ("dram", [8, 128, 128], "float32"),
    "la": ("dram", [9, 128, 128], "float32"),
    "res": ("dram", [3, 128, 128], "float32"),
}
SEMAPHORES = ["st", "snt", "ra", "rb", "rp", "arr"] + ["f%d" % c for c in range(8)] + ["l%d" % c for c in range(8)]


def sem_f(T, c):
    return [T.sem.f0, T.sem.f1, T.sem.f2, T.sem.f3, T.sem.f4, T.sem.f5, T.sem.f6, T.sem.f7][c]


def sem_l(T, c):
    return [T.sem.l0, T.sem.l1, T.sem.l2, T.sem.l3, T.sem.l4, T.sem.l5, T.sem.l6, T.sem.l7][c]


def groups(k):
    rot = [(k + 1 + i) % 8 for i in range(8)]
    return [rot[c * JPER:(c + 1) * JPER] for c in range(E)]


def early(s, j):
    return j not in groups(s)[-1]


def fwd_plan(k):
    out, n = [], 0
    for js in groups(k):
        per = {}
        for j in js:
            if j != k:
                per.setdefault(FWD[n % len(FWD)], []).append(j)
                n += 1
        out.append(per)
    return out


def fwd_engines(n):
    e = 8
    while e * n > 8:
        e //= 2
    return e


def fwd_count(s, j):
    for per in fwd_plan(s):
        for lst in per.values():
            if j in lst:
                return fwd_engines(len(lst))
    return 0


def xfer(topo, dst_core, mask, sem, src, dst):
    rid, pid, se = topo.addr(dst_core)
    return bass.RemoteDMATransfer(dst_ids=[bass.DstId(rid=rid, pnc=pid)], dma_engine_mask=mask, remote_sem=sem,
                                  src=src, dst=dst)


def fold(topo, dst_core, mask, sem, srcs, dst):
    rid, pid, se = topo.addr(dst_core)
    return bass.RemoteDMATransfer(dst_ids=[bass.DstId(rid=rid, pnc=pid)], dma_engine_mask=mask, remote_sem=sem,
                                  srcs=srcs, dsts=[dst], alu_op=1)


def rank_core(g, T, topo, k, p):
    base = (2 * k + p) * 8
    gs = groups(k)
    plan = fwd_plan(k)
    where = {}
    for c in range(E):
        for f, lst in plan[c].items():
            for j in lst:
                where[j] = f

    def load(c):
        runs = []
        for j in sorted(gs[c]):
            if runs and runs[-1][1] == j:
                runs[-1][1] = j + 1
            else:
                runs.append([j, j + 1])
        for a, b in runs:
            g.dma_start(T.xs[:, 256 * a:256 * b], T.x[:, 256 * a:256 * b]).then_inc(sem_l(T, c), 16)
        return 16 * len(runs)

    def block(b):
        return T.xs[:, 128 * b:128 * (b + 1)]

    loaded = [load(0)]
    for c in range(E):
        if c + 1 < E:
            loaded.append(load(c + 1))
        g.wait_ge(sem_l(T, c), loaded[c])
        tr = []
        for i, j in enumerate(gs[c]):
            m = ((1 << E) - 1) << (i * E)
            tr.append(xfer(topo, (2 * j + p) * 8 + (PB if early(k, j) else FB), m, T.sem.arr, block(2 * j + 1 - p),
                           T.la[k]))
            if j == k:
                tr.append(xfer(topo, base + FA, m << 8, T.sem.arr, block(2 * j + p), T.la[k]))
            else:
                tr.append(xfer(topo, base + where[j], m << 8, sem_f(T, c), block(2 * j + p), T.fw[j]))
        g.remote_dma_fused(tr, local_sem=T.sem.snt)
    add = mybir.AluOpType.add
    g.wait_ge(T.sem.rp, 8)
    g.dma_start(T.y[:], T.res[0]).then_inc(T.sem.st, 16)
    g.wait_ge(T.sem.rb, 8)
    g.wait_ge(T.sem.st, 16)
    g.dma_start(T.y[:], T.res[1], accum_op=add, max_dma_last_dim=8192).then_inc(T.sem.st, 16)
    g.wait_ge(T.sem.ra, 16)
    g.wait_ge(T.sem.st, 32)
    g.dma_start(T.y[:], T.res[2], accum_op=add, max_dma_last_dim=8192).then_inc(T.sem.st, 16)
    g.wait_ge(T.sem.snt, 16 * E)
    g.wait_ge(T.sem.st, 48)


def helper_core(g, T, topo, k, p, me):
    base = (2 * k + p) * 8
    sent = 0
    if me in FWD:
        plan = fwd_plan(k)
        for c in range(E):
            lst = plan[c].get(me, [])
            if not lst:
                continue
            g.wait_ge(sem_f(T, c), E * len(lst))
            e = fwd_engines(len(lst))
            tr = [xfer(topo, (2 * j + p) * 8 + (PA if early(k, j) else FA), ((1 << e) - 1) << (i * e), T.sem.arr,
                       T.fw[j], T.la[k]) for i, j in enumerate(lst)]
            g.remote_dma_fused(tr, local_sem=T.sem.snt)
            sent += e * len(lst)
    first = [s for s in range(8) if early(s, k)]
    rest = [s for s in range(8) if s not in first]
    if me == PB or me == FB:
        srcs = first if me == PB else rest
        g.wait_ge(T.sem.arr, E * len(srcs))
        g.remote_dma_fused([fold(topo, (base ^ 8) + 1, 0x00FF, T.sem.rp if me == PB else T.sem.rb,
                                 [T.la[s] for s in srcs], T.res[0 if me == PB else 1])], local_sem=T.sem.snt)
        sent += 8
    if me == PA:
        g.wait_ge(T.sem.arr, sum(fwd_count(s, k) for s in first))
        g.remote_dma_fused([fold(topo, base + FA, 0xFFFF, T.sem.arr, [T.la[s] for s in first], T.la[8])],
                           local_sem=T.sem.snt)
        sent += 16
    if me == FA:
        g.wait_ge(T.sem.arr, sum(E if s == k else fwd_count(s, k) for s in rest) + 16)
        g.remote_dma_fused([fold(topo, base + 1, 0xFFFF, T.sem.ra, [T.la[s] for s in rest] + [T.la[8]], T.res[2])],
                           local_sem=T.sem.snt)
        sent += 16
    if sent:
        g.wait_ge(T.sem.snt, sent)


def rank_program(g, core, T, topo):
    ch, me = core // 8, core % 8
    if me == 1:
        rank_core(g, T, topo, ch // 2, ch % 2)
    else:
        helper_core(g, T, topo, ch // 2, ch % 2, me)
